import numpy as np
CORES = [88,89,90,91,92,93,94,95,96,97,98,99,100,101,102,103]
N = 16
WIDTHS = [2,4,4,16,0,2,8,4,0,4,32,2,4,16,2,0]
OFF = [0,2,6,10,26,26,28,36,40,40,44,76,78,82,98,100]
C = 100
def setup_inputs(rng):
    return {"x": rng.standard_normal((N, 128, C), dtype=np.float32)}
def reference(x):
    s = x.sum(axis=0, dtype=np.float64).astype(x.dtype)
    YW = max(WIDTHS)
    y = np.full((N, 128, YW), np.nan, x.dtype)
    for r in range(N):
        y[r][:, :WIDTHS[r]] = s[:, OFF[r]:OFF[r] + WIDTHS[r]]
    return {"y": y}

@@ -1,0 +1,121 @@
+from concourse.bass import DstId, RemoteDMATransfer
+
+SLOT = 16
+
+SCRATCH = {
+    "xs": ("sbuf", [128, 100], "float32"),
+    "land": ("sbuf", [128, 8 * SLOT], "float32"),
+    "rem": ("sbuf", [128, SLOT], "float32"),
+    "res": ("sbuf", [128, 32], "float32"),
+}
+SEMAPHORES = ["loaded", "arrived", "rem", "fin", "sent", "stored"]
+
+PORT = (2, 3, 6, 7)
+INNER = (0, 1, 4, 5)
+
+
+def _cuts(lo, hi, n):
+    w = hi - lo
+    return [(lo + w * i // n, lo + w * (i + 1) // n) for i in range(n)]
+
+
+def _perms(items):
+    if len(items) <= 1:
+        return [list(items)]
+    out = []
+    for i in range(len(items)):
+        for p in _perms(items[:i] + items[i + 1:]):
+            out.append([items[i]] + p)
+    return out
+
+
+def _plan(T):
+    W, OFF = T.tables["WIDTHS"], T.tables["OFF"]
+    plan = []
+    for h in (0, 1):
+        ranks = list(range(8 * h, 8 * h + 8))
+        lo, hi = OFF[ranks[0]], OFF[ranks[-1]] + W[ranks[-1]]
+        cuts = _cuts(lo, hi, 4)
+        pick = None
+        for p in _perms(cuts):
+            ok = True
+            for k, (a, b) in zip(INNER, p):
+                r = 8 * h + k
+                if max(a, OFF[r]) < min(b, OFF[r] + W[r]):
+                    ok = False
+            if ok:
+                pick = p
+                break
+        plan.append([(a, b, INNER[i], PORT[i]) for i, (a, b) in enumerate(pick)])
+    return plan
+
+
+def rank_program(g, core, T, topo):
+    rank = T.rank_of(core)
+    if rank is None:
+        return
+    W, OFF = T.tables["WIDTHS"], T.tables["OFF"]
+    plan = _plan(T)
+    h, k = rank // 8, rank % 8
+    base = T.cores[8 * h]
+    obase = T.cores[8 * (1 - h)]
+    sem = T.sem
+
+    rng = {}
+    for a, b, inner, port in plan[h]:
+        rng[inner] = (a, b)
+    for a, b, inner, port in plan[1 - h]:
+        rng[port] = (a, b)
+
+    g.dma_start(T.xs[:], T.x[:]).then_inc(sem.loaded, 16)
+    g.wait_ge(sem.loaded, 16)
+
+    sent = 0
+    for j in range(8):
+        if j == k:
+            continue
+        a, b = rng[j]
+        rid, pid, _se = topo.addr(base + j)
+        g.remote_dma(T.land[:, k * SLOT:k * SLOT + b - a], T.xs[:, a:b], sem.arrived, sem.sent, pid, rid,
+                     topo.mask(core, base + j))
+        sent += 16
+
+    a, b = rng[k]
+
+    def parts(c0, c1):
+        s = [T.land[:, j * SLOT + c0 - a:j * SLOT + c1 - a] for j in range(8) if j != k]
+        return s + [T.xs[:, c0:c1]]
+
+    g.wait_ge(sem.arrived, 7 * 16)
+    if k in PORT:
+        inner = [i for (a2, b2, i, p) in plan[1 - h] if p == k][0]
+        dst = obase + inner
+        rid, pid, _se = topo.addr(dst)
+        g.remote_dma_fused([RemoteDMATransfer(dst_ids=[DstId(rid=rid, pnc=pid)], dma_engine_mask=topo.mask(core, dst),
+                                              remote_sem=sem.rem, srcs=parts(a, b), dsts=[T.rem[:, 0:b - a]],
+                                              alu_op=1)], local_sem=sem.sent)
+        sent += 8
+    else:
+        g.wait_ge(sem.rem, 8)
+        for r in range(8 * h, 8 * h + 8):
+            c0, c1 = max(a, OFF[r]), min(b, OFF[r] + W[r])
+            if c0 >= c1:
+                continue
+            dst = T.cores[r]
+            rid, pid, _se = topo.addr(dst)
+            g.remote_dma_fused([RemoteDMATransfer(dst_ids=[DstId(rid=rid, pnc=pid)],
+                                                  dma_engine_mask=topo.mask(core, dst), remote_sem=sem.fin,
+                                                  srcs=parts(c0, c1) + [T.rem[:, c0 - a:c1 - a]],
+                                                  dsts=[T.res[:, c0 - OFF[r]:c1 - OFF[r]]], alu_op=1)],
+                               local_sem=sem.sent)
+            sent += 16
+
+    if W[rank] > 0:
+        n = 0
+        for a2, b2, inner, port in plan[h]:
+            if max(a2, OFF[rank]) < min(b2, OFF[rank] + W[rank]):
+                n += 1
+        g.wait_ge(sem.fin, 16 * n)
+        g.dma_start(T.y[:, 0:W[rank]], T.res[:, 0:W[rank]]).then_inc(sem.stored, 16)
+        g.wait_ge(sem.stored, 16)
+    g.wait_ge(sem.sent, sent)

@@ -1,22 +1,16 @@
 from concourse.bass import DstId, RemoteDMATransfer
 
-SLOT = 16
+HALF = (13, 7, 18, 12)
 
-SCRATCH = {
-    "xs": ("sbuf", [128, 100], "float32"),
-    "land": ("sbuf", [128, 8 * SLOT], "float32"),
-    "rem": ("sbuf", [128, SLOT], "float32"),
-    "res": ("sbuf", [128, 32], "float32"),
-}
-SEMAPHORES = ["loaded", "arrived", "rem", "fin", "sent", "stored"]
+SCRATCH = {}
+for _i, _n in enumerate(HALF):
+    SCRATCH["g%d" % _i] = ("dram", [2, 128, _n], "float32")
+    SCRATCH["l%d" % _i] = ("dram", [8, 128, _n], "float32")
+    SCRATCH["r%d" % _i] = ("dram", [128, _n], "float32")
+    SCRATCH["f%d" % _i] = ("dram", [256, _n], "float32")
+SEMAPHORES = ["ld0", "ld1", "ld2", "ld3", "arrived", "rem", "fin", "sent", "stored"]
 
-PORT = (2, 3, 6, 7)
 INNER = (0, 1, 4, 5)
-
-
-def _cuts(lo, hi, n):
-    w = hi - lo
-    return [(lo + w * i // n, lo + w * (i + 1) // n) for i in range(n)]
 
 
 def _perms(items):
@@ -31,23 +25,29 @@ def _perms(items):
 
 def _plan(T):
     W, OFF = T.tables["WIDTHS"], T.tables["OFF"]
-    plan = []
+    groups = []
     for h in (0, 1):
-        ranks = list(range(8 * h, 8 * h + 8))
-        lo, hi = OFF[ranks[0]], OFF[ranks[-1]] + W[ranks[-1]]
-        cuts = _cuts(lo, hi, 4)
-        pick = None
-        for p in _perms(cuts):
-            ok = True
-            for k, (a, b) in zip(INNER, p):
-                r = 8 * h + k
-                if max(a, OFF[r]) < min(b, OFF[r] + W[r]):
-                    ok = False
-            if ok:
-                pick = p
-                break
-        plan.append([(a, b, INNER[i], PORT[i]) for i, (a, b) in enumerate(pick)])
-    return plan
+        owners = [r for r in range(8 * h, 8 * h + 8) if W[r] > 0]
+        best = None
+        for s in range(1, len(owners)):
+            A, B = owners[:s], owners[s:]
+            wa, wb = sum(W[r] for r in A), sum(W[r] for r in B)
+            if wa % 2 or wb % 2:
+                continue
+            for p in _perms(list(INNER)):
+                if p[0] > p[1] or p[2] > p[3]:
+                    continue
+                if [q for q in p[:2] if 8 * h + q in A] or [q for q in p[2:] if 8 * h + q in B]:
+                    continue
+                cost = len(A) * wa + len(B) * wb
+                if best is None or cost < best[0]:
+                    best = (cost, A, B, wa, wb, p)
+        cost, A, B, wa, wb, p = best
+        groups.append((h, OFF[A[0]], wa // 2, A, p[:2], (2, 6)))
+        groups.append((h, OFF[B[0]], wb // 2, B, p[2:], (3, 7)))
+    if tuple(G[2] for G in groups) != HALF:
+        raise ValueError("HALF does not fit the tables")
+    return groups
 
 
 def rank_program(g, core, T, topo):
@@ -55,67 +55,69 @@ def rank_program(g, core, T, topo):
     if rank is None:
         return
     W, OFF = T.tables["WIDTHS"], T.tables["OFF"]
-    plan = _plan(T)
+    groups = _plan(T)
     h, k = rank // 8, rank % 8
     base = T.cores[8 * h]
     obase = T.cores[8 * (1 - h)]
     sem = T.sem
 
-    rng = {}
-    for a, b, inner, port in plan[h]:
-        rng[inner] = (a, b)
-    for a, b, inner, port in plan[1 - h]:
-        rng[port] = (a, b)
+    def did(c):
+        rid, pid, _se = topo.addr(c)
+        return DstId(rid=rid, pnc=pid)
 
-    g.dma_start(T.xs[:], T.x[:]).then_inc(sem.loaded, 16)
-    g.wait_ge(sem.loaded, 16)
+    order = [i for i in range(4) if groups[i][0] != h] + [i for i in range(4) if groups[i][0] == h]
+
+    for t, i in enumerate(order):
+        gh, lo, n, owners, fin, port = groups[i]
+        q = (g.sync, g.scalar)[t % 2]
+        q.dma_start(T["g%d" % i][:], T.x[:, lo:lo + 2 * n]).then_inc(sem["ld%d" % i], 16)
 
     sent = 0
-    for j in range(8):
-        if j == k:
-            continue
-        a, b = rng[j]
-        rid, pid, _se = topo.addr(base + j)
-        g.remote_dma(T.land[:, k * SLOT:k * SLOT + b - a], T.xs[:, a:b], sem.arrived, sem.sent, pid, rid,
-                     topo.mask(core, base + j))
-        sent += 16
+    mine = None
+    for i in order:
+        gh, lo, n, owners, fin, port = groups[i]
+        red = fin if gh == h else port
+        g.wait_ge(sem["ld%d" % i], 16)
+        trs = []
+        for j in (0, 1):
+            if red[j] == k:
+                mine = (i, j)
+                continue
+            trs.append(RemoteDMATransfer(dst_ids=[did(base + red[j])], dma_engine_mask=0x00FF << (8 * j),
+                                         remote_sem=sem.arrived, src=T["g%d" % i][j], dst=T["l%d" % i][k]))
+            sent += 8
+        g.remote_dma_fused(trs, local_sem=sem.sent)
 
-    a, b = rng[k]
-
-    def parts(c0, c1):
-        s = [T.land[:, j * SLOT + c0 - a:j * SLOT + c1 - a] for j in range(8) if j != k]
-        return s + [T.xs[:, c0:c1]]
-
-    g.wait_ge(sem.arrived, 7 * 16)
-    if k in PORT:
-        inner = [i for (a2, b2, i, p) in plan[1 - h] if p == k][0]
-        dst = obase + inner
-        rid, pid, _se = topo.addr(dst)
-        g.remote_dma_fused([RemoteDMATransfer(dst_ids=[DstId(rid=rid, pnc=pid)], dma_engine_mask=topo.mask(core, dst),
-                                              remote_sem=sem.rem, srcs=parts(a, b), dsts=[T.rem[:, 0:b - a]],
-                                              alu_op=1)], local_sem=sem.sent)
+    i, j = mine
+    gh, lo, n, owners, fin, port = groups[i]
+    srcs = [T["l%d" % i][kk] for kk in range(8) if kk != k] + [T["g%d" % i][j]]
+    g.wait_ge(sem.arrived, 7 * 8)
+    if gh != h:
+        dst = obase + fin[j]
+        g.remote_dma_fused([RemoteDMATransfer(dst_ids=[did(dst)], dma_engine_mask=topo.mask(core, dst),
+                                              remote_sem=sem.rem, srcs=srcs, dsts=[T["r%d" % i][:]], alu_op=1)],
+                           local_sem=sem.sent)
         sent += 8
     else:
         g.wait_ge(sem.rem, 8)
-        for r in range(8 * h, 8 * h + 8):
-            c0, c1 = max(a, OFF[r]), min(b, OFF[r] + W[r])
-            if c0 >= c1:
-                continue
-            dst = T.cores[r]
-            rid, pid, _se = topo.addr(dst)
-            g.remote_dma_fused([RemoteDMATransfer(dst_ids=[DstId(rid=rid, pnc=pid)],
-                                                  dma_engine_mask=topo.mask(core, dst), remote_sem=sem.fin,
-                                                  srcs=parts(c0, c1) + [T.rem[:, c0 - a:c1 - a]],
-                                                  dsts=[T.res[:, c0 - OFF[r]:c1 - OFF[r]]], alu_op=1)],
-                               local_sem=sem.sent)
-            sent += 16
+        g.remote_dma_fused([RemoteDMATransfer(dst_ids=[did(T.cores[r]) for r in owners], dma_engine_mask=0xFFFF,
+                                              remote_sem=sem.fin, srcs=srcs + [T["r%d" % i][:]],
+                                              dsts=[T["f%d" % i][128 * j:128 * j + 128, :] for r in owners],
+                                              alu_op=1)], local_sem=sem.sent)
+        sent += 16
 
     if W[rank] > 0:
-        n = 0
-        for a2, b2, inner, port in plan[h]:
-            if max(a2, OFF[rank]) < min(b2, OFF[rank] + W[rank]):
-                n += 1
-        g.wait_ge(sem.fin, 16 * n)
-        g.dma_start(T.y[:, 0:W[rank]], T.res[:, 0:W[rank]]).then_inc(sem.stored, 16)
-        g.wait_ge(sem.stored, 16)
+        i = [t for t in range(4) if rank in groups[t][3]][0]
+        gh, lo, n, owners, fin, port = groups[i]
+        a, b = OFF[rank] - lo, OFF[rank] - lo + W[rank]
+        stored = 0
+        for hf in (0, 1):
+            c0, c1 = max(a, hf * n), min(b, (hf + 1) * n)
+            if c0 >= c1:
+                continue
+            q = (g.sync, g.scalar)[hf]
+            q.wait_ge(sem.fin, 2 * 16)
+            q.dma_start(T.y[:, c0 - a:c1 - a], T["f%d" % i][hf::2, c0 - hf * n:c1 - hf * n]).then_inc(sem.stored, 16)
+            stored += 16
+        g.wait_ge(sem.stored, stored)
     g.wait_ge(sem.sent, sent)

from concourse.bass import DstId, RemoteDMATransfer

HALF = (13, 7, 18, 12)

SCRATCH = {}
for _i, _n in enumerate(HALF):
    SCRATCH["g%d" % _i] = ("dram", [2, 128, _n], "float32")
    SCRATCH["l%d" % _i] = ("dram", [8, 128, _n], "float32")
    SCRATCH["r%d" % _i] = ("dram", [128, _n], "float32")
    SCRATCH["f%d" % _i] = ("dram", [256, _n], "float32")
SEMAPHORES = ["ld0", "ld1", "ld2", "ld3", "arrived", "rem", "fin", "sent", "stored"]

INNER = (0, 1, 4, 5)


def _perms(items):
    if len(items) <= 1:
        return [list(items)]
    out = []
    for i in range(len(items)):
        for p in _perms(items[:i] + items[i + 1:]):
            out.append([items[i]] + p)
    return out


def _plan(T):
    W, OFF = T.tables["WIDTHS"], T.tables["OFF"]
    groups = []
    for h in (0, 1):
        owners = [r for r in range(8 * h, 8 * h + 8) if W[r] > 0]
        best = None
        for s in range(1, len(owners)):
            A, B = owners[:s], owners[s:]
            wa, wb = sum(W[r] for r in A), sum(W[r] for r in B)
            if wa % 2 or wb % 2:
                continue
            for p in _perms(list(INNER)):
                if p[0] > p[1] or p[2] > p[3]:
                    continue
                if [q for q in p[:2] if 8 * h + q in A] or [q for q in p[2:] if 8 * h + q in B]:
                    continue
                cost = len(A) * wa + len(B) * wb
                if best is None or cost < best[0]:
                    best = (cost, A, B, wa, wb, p)
        cost, A, B, wa, wb, p = best
        groups.append((h, OFF[A[0]], wa // 2, A, p[:2], (2, 6)))
        groups.append((h, OFF[B[0]], wb // 2, B, p[2:], (3, 7)))
    if tuple(G[2] for G in groups) != HALF:
        raise ValueError("HALF does not fit the tables")
    return groups


def rank_program(g, core, T, topo):
    rank = T.rank_of(core)
    if rank is None:
        return
    W, OFF = T.tables["WIDTHS"], T.tables["OFF"]
    groups = _plan(T)
    h, k = rank // 8, rank % 8
    base = T.cores[8 * h]
    obase = T.cores[8 * (1 - h)]
    sem = T.sem

    def did(c):
        rid, pid, _se = topo.addr(c)
        return DstId(rid=rid, pnc=pid)

    order = [i for i in range(4) if groups[i][0] != h] + [i for i in range(4) if groups[i][0] == h]

    for t, i in enumerate(order):
        gh, lo, n, owners, fin, port = groups[i]
        q = (g.sync, g.scalar)[t % 2]
        q.dma_start(T["g%d" % i][:], T.x[:, lo:lo + 2 * n]).then_inc(sem["ld%d" % i], 16)

    sent = 0
    mine = None
    for i in order:
        gh, lo, n, owners, fin, port = groups[i]
        red = fin if gh == h else port
        g.wait_ge(sem["ld%d" % i], 16)
        trs = []
        for j in (0, 1):
            if red[j] == k:
                mine = (i, j)
                continue
            trs.append(RemoteDMATransfer(dst_ids=[did(base + red[j])], dma_engine_mask=0x00FF << (8 * j),
                                         remote_sem=sem.arrived, src=T["g%d" % i][j], dst=T["l%d" % i][k]))
            sent += 8
        g.remote_dma_fused(trs, local_sem=sem.sent)

    i, j = mine
    gh, lo, n, owners, fin, port = groups[i]
    srcs = [T["l%d" % i][kk] for kk in range(8) if kk != k] + [T["g%d" % i][j]]
    g.wait_ge(sem.arrived, 7 * 8)
    if gh != h:
        dst = obase + fin[j]
        g.remote_dma_fused([RemoteDMATransfer(dst_ids=[did(dst)], dma_engine_mask=topo.mask(core, dst),
                                              remote_sem=sem.rem, srcs=srcs, dsts=[T["r%d" % i][:]], alu_op=1)],
                           local_sem=sem.sent)
        sent += 8
    else:
        g.wait_ge(sem.rem, 8)
        g.remote_dma_fused([RemoteDMATransfer(dst_ids=[did(T.cores[r]) for r in owners], dma_engine_mask=0xFFFF,
                                              remote_sem=sem.fin, srcs=srcs + [T["r%d" % i][:]],
                                              dsts=[T["f%d" % i][128 * j:128 * j + 128, :] for r in owners],
                                              alu_op=1)], local_sem=sem.sent)
        sent += 16

    if W[rank] > 0:
        i = [t for t in range(4) if rank in groups[t][3]][0]
        gh, lo, n, owners, fin, port = groups[i]
        a, b = OFF[rank] - lo, OFF[rank] - lo + W[rank]
        stored = 0
        for hf in (0, 1):
            c0, c1 = max(a, hf * n), min(b, (hf + 1) * n)
            if c0 >= c1:
                continue
            q = (g.sync, g.scalar)[hf]
            q.wait_ge(sem.fin, 2 * 16)
            q.dma_start(T.y[:, c0 - a:c1 - a], T["f%d" % i][hf::2, c0 - hf * n:c1 - hf * n]).then_inc(sem.stored, 16)
            stored += 16
        g.wait_ge(sem.stored, stored)
    g.wait_ge(sem.sent, sent)
